import numpy as np
import ml_dtypes


def mxq(x, axis, fmt="e4m3"):
    dtype, down = {"e4m3": (ml_dtypes.float8_e4m3fn, 7), "e5m2": (ml_dtypes.float8_e5m2, 14)}[fmt]
    v = np.moveaxis(np.asarray(x, np.float32).astype(ml_dtypes.bfloat16).astype(np.float64), axis, -1)
    blocks = v.reshape(v.shape[:-1] + (-1, 32))
    amax = np.abs(blocks).max(-1, keepdims=True)
    byte = np.maximum(np.where(amax > 0, np.frexp(amax)[1] - 1 + 127, 0) - down, 1)
    scale = np.exp2(byte - 127.0)
    codes = (blocks / scale).astype(np.float32).astype(dtype).astype(np.float64)
    return np.moveaxis((codes * scale).reshape(v.shape), -1, axis)


WIDE = False


def mx_kscale(k):
    if not WIDE:
        return np.ones(k)
    levels = np.array([30, -30])
    if k % 512:
        return np.exp2(np.random.permutation(np.resize(levels, k // 32))).repeat(32)
    a = np.empty((k // 512, 16))
    for p in range(k // 512):
        a[p, :8] = np.random.permutation(np.resize(levels, 8))
        for g in range(8):
            far = levels[np.abs(levels - a[p, g]) >= 10]
            a[p, g + 8] = far[np.random.randint(len(far))]
    return np.exp2(a.ravel()).repeat(32)


BF16 = ml_dtypes.bfloat16


def bf(x):
    return np.asarray(x, np.float32).astype(BF16)


def f64(x):
    return np.asarray(x).astype(np.float64)


E2M1 = np.array([0.0, 0.5, 1.0, 1.5, 2.0, 3.0, 4.0, 6.0, -0.0, -0.5, -1.0, -1.5, -2.0, -3.0, -4.0, -6.0])


def pack_weight(w, fmt):
    k, n = w.shape
    w = f64(bf(w)).reshape(k // 32, 32, n)
    amax = np.abs(w).max(1)
    if fmt in ("e4m3", "e5m2"):
        byte = np.frexp(amax)[1] - 1 + 127 - (7 if fmt == "e4m3" else 14)
    else:
        mant, ex = np.frexp(amax / 6.0)
        byte = np.where(mant > 0.5, ex, ex - 1) + 127
    byte = np.clip(np.where(amax > 0, byte, 1), 1, 254)
    scaled = (w * np.exp2(127.0 - byte)[:, None, :]).reshape(k, n).astype(np.float32)
    by_word = np.ascontiguousarray(scaled.reshape(k // 512, 128, 4, n).transpose(0, 1, 3, 2))
    if fmt in ("e4m3", "e5m2"):
        words = by_word.astype(ml_dtypes.float8_e4m3fn if fmt == "e4m3" else ml_dtypes.float8_e5m2).view(np.uint8)
    else:
        c = by_word.astype(ml_dtypes.float4_e2m1fn).view(np.uint8) & 0xF
        words = c[..., 0::2] | (c[..., 1::2] << 4)
    return np.ascontiguousarray(words), np.ascontiguousarray(byte.astype(np.uint8).reshape(k // 512, 16, n))


def unpack_weight(words, scales, fmt):
    g, p, n, _ = words.shape
    if fmt in ("e4m3", "e5m2"):
        vals = np.ascontiguousarray(words).view(ml_dtypes.float8_e4m3fn if fmt == "e4m3" else ml_dtypes.float8_e5m2).astype(np.float64)
    else:
        nib = np.empty((g, p, n, 4), np.uint8)
        nib[..., 0::2] = words & 0xF
        nib[..., 1::2] = words >> 4
        vals = E2M1[nib]
    vals = vals * np.repeat(np.exp2(scales.astype(np.float64) - 127.0), 8, axis=1)[..., None]
    return vals.transpose(0, 1, 3, 2).reshape(g * 512, n)


H, D, M, N = 8, 512, 512, 2048


def setup_inputs():
    s = mx_kscale(H * D)
    G = np.random.standard_t(5, (H * D, N)) * s[:, None]
    g_words, g_scales = pack_weight(G, "e5m2")
    jac = np.random.standard_normal((H, D, M)) / np.sqrt(H * D)
    return {"g_words": g_words,
            "g_scales": g_scales,
            "jac": bf(jac / s.reshape(H, D, 1)),
            "c": bf(1 + 0.1 * np.random.standard_normal(M)),
            "r": bf(1 + 0.1 * np.random.standard_normal(M)),
            "u": bf(np.random.standard_normal((M, N)))}


def reference(g_words, g_scales, jac, c, r, u):
    G = unpack_weight(g_words, g_scales, "e5m2")
    B = mxq(f64(jac).reshape(H * D, M), 0, "e4m3")
    pulled = B.T @ G
    return f64(c)[:, None] * pulled + f64(r)[:, None] * f64(u)

@@ -1,0 +1,192 @@
+from contextlib import ExitStack
+
+import concourse.mybir as mybir
+
+H, D, M, N = 8, 512, 512, 2048
+FLOPS = 2 * H * D * M * N
+
+F32 = mybir.dt.float32
+BF16 = mybir.dt.bfloat16
+I32 = mybir.dt.int32
+U32 = mybir.dt.uint32
+U8 = mybir.dt.uint8
+E4M3 = mybir.dt.float8_e4m3fn_x4
+E5M2 = mybir.dt.float8_e5m2_x4
+COPY = mybir.ActivationFunctionType.Copy
+MULT = mybir.AluOpType.mult
+ADD = mybir.AluOpType.add
+
+P = 128
+PACK = 4
+MT = M // P
+NT = 512
+HALF = N // 2
+MH = M // 2
+SCALE_RUNS = (((0, 3), (3, 8)), ((0, 4), (4, 8)))
+TOGETHER = 6
+
+
+def tile_held_control_gradient_e2_kernel(tc, g_words, g_scales, jac, c, r, u, out):
+    nc = tc.nc
+    with ExitStack() as ctx:
+        keep = ctx.enter_context(tc.tile_pool(name="keep", bufs=1))
+        stage = ctx.enter_context(tc.tile_pool(name="stage", bufs=3))
+        psum = ctx.enter_context(tc.psum_pool(name="psum", bufs=1))
+        ctx.enter_context(tc.manual_schedule())
+
+        scale_rows = g_scales.bitcast(I32).rearrange("g (q s) n -> s q g n", s=4)
+
+        planes = {}
+        for half in range(2):
+            for g0, g1 in SCALE_RUNS[half]:
+                plane = keep.tile([P, g1 - g0, HALF], U8, name="plane%d_%d" % (half, g0), align_bytes=64)
+                nc.vector.memset(plane[:].bitcast(I32), 0)
+                for g in range(g0, g1):
+                    planes[half, g] = (plane, g - g0)
+        cr_rows = keep.tile([P, 32], BF16, name="cr_rows", align_bytes=64)
+        nc.vector.memset(cr_rows[:], 0.0)
+
+        def load_scales(half, run):
+            g0, g1 = SCALE_RUNS[half][run]
+            plane = planes[half, g0][0]
+            words = slice(half * HALF // 4, (half + 1) * HALF // 4)
+            for s in range(4):
+                nc.sync.dma_start(out=plane[s:P:32, :, :].bitcast(I32), in_=scale_rows[s, :, g0:g1, words])
+
+        g_codes = {}
+
+        def load_g(half, g):
+            codes = keep.tile([P, HALF], U32, name="g%d_%d" % (half, g), align_bytes=64)
+            src = g_words[g].rearrange("p n t -> p (n t)")[:, half * HALF * PACK:(half + 1) * HALF * PACK]
+            nc.sync.dma_start(out=codes[:].bitcast(I32), in_=src.bitcast(I32))
+            g_codes[half, g] = codes
+
+        raws = {}
+
+        def load_jac(g):
+            raw = keep.tile([P, PACK, M], BF16, name="raw%d" % g)
+            nc.sync.dma_start(out=raw[:], in_=jac[g].rearrange("(p j) m -> p j m", j=PACK))
+            raws[g] = raw
+
+        def load_cr(t):
+            nc.sync.dma_start(out=cr_rows[t:P:32, :], in_=c.rearrange("(t q j) -> t q j", t=MT, q=4)[t])
+            nc.sync.dma_start(out=cr_rows[MT + t:P:32, :], in_=r.rearrange("(t q j) -> t q j", t=MT, q=4)[t])
+
+        b_codes = {}
+
+        def quantize_jac(g):
+            grouped = []
+            for mh in range(2):
+                tile = stage.tile([P, MH, PACK], BF16, name="grouped%d" % mh, align_bytes=64)
+                dst = tile[:].rearrange("p (a i) j -> p a j i", i=4)
+                src = raws[g][:, :, mh * MH:(mh + 1) * MH].rearrange("p j (a i) -> p a j i", i=4)
+                if mh == 0:
+                    nc.vector.tensor_copy(out=dst, in_=src)
+                else:
+                    nc.scalar.activation(out=dst, in_=src, func=COPY)
+                grouped.append(tile)
+            for mh in range(2):
+                codes = keep.tile([P, MH], U32, name="bc%d_%d" % (g, mh), align_bytes=64)
+                scales = keep.tile([P, MH], U8, name="bs%d_%d" % (g, mh), align_bytes=64)
+                nc.vector.quantize_mx(
+                    out=codes[:].bitcast(E4M3),
+                    scales=scales[:],
+                    in_=grouped[mh][:].rearrange("p m j -> p (m j)"),
+                )
+                b_codes[g, mh] = (codes, scales)
+
+        def multiply(acc, half, g, mt, nt):
+            codes, scales = b_codes[g, mt // 2]
+            m_cols = slice((mt % 2) * P, (mt % 2 + 1) * P)
+            n_cols = slice(nt * NT, (nt + 1) * NT)
+            plane, slot = planes[half, g]
+            nc.tensor.matmul_mx(
+                out=acc[:],
+                lhsT=codes[:, m_cols].bitcast(E4M3),
+                lhsT_scale=scales[:, m_cols],
+                rhs=g_codes[half, g][:, n_cols].bitcast(E5M2),
+                rhs_scale=plane[:, slot, n_cols],
+                start=(g == 0),
+                stop=(g == H - 1),
+            )
+
+        banks = [(mt, nt) for mt in range(MT) for nt in range(2)]
+
+        accs = {}
+        for mt, nt in banks:
+            accs[mt, nt] = psum.tile([P, NT], F32, name="acc%d_%d" % (mt, nt))
+        cr_cols = keep.tile([P, 32], BF16, name="cr_cols", align_bytes=64)
+        cr = keep.tile([P, 2 * MT], F32, name="cr")
+        for g in range(H):
+            load_jac(g)
+            if g == 0:
+                load_scales(0, 0)
+            load_g(0, g)
+            if g == 1:
+                load_scales(0, 1)
+            if 2 <= g < 2 + MT:
+                load_cr(g - 2)
+            quantize_jac(g)
+            if g == H - 1:
+                nc.vector.transpose(out=cr_cols[:], in_=cr_rows[:])
+                nc.vector.tensor_copy(out=cr[:], in_=cr_cols[:, 0:2 * MT])
+            for mt, nt in banks:
+                multiply(accs[mt, nt], 0, g, mt, nt)
+
+        results = {}
+        for half in range(2):
+            for mt in range(MT):
+                results[half, mt] = keep.tile([P, HALF], F32, name="res%d_%d" % (half, mt))
+        for mt, nt in banks:
+            dst = results[0, mt][:, nt * NT:(nt + 1) * NT]
+            if nt == 0:
+                nc.scalar.activation(out=dst, in_=accs[mt, nt][:], func=COPY, scale=cr[:, mt:mt + 1])
+            else:
+                nc.vector.tensor_scalar(out=dst, in0=accs[mt, nt][:], scalar1=cr[:, mt:mt + 1], scalar2=None, op0=MULT)
+
+        def load_u(mt):
+            u_rows = keep.tile([P, N], BF16, name="u%d" % mt)
+            nc.sync.dma_start(out=u_rows[:], in_=u[mt * P:(mt + 1) * P, :])
+            r_col = cr[:, MT + mt:MT + mt + 1]
+            nc.vector.scalar_tensor_tensor(
+                out=results[0, mt][:], in0=u_rows[:, 0:HALF], scalar=r_col, in1=results[0, mt][:], op0=MULT, op1=ADD
+            )
+            nc.scalar.activation(out=results[1, mt][:], in_=u_rows[:, HALF:N], func=COPY, scale=r_col)
+
+        def store(half, mt):
+            nc.sync.dma_start(out=out[mt * P:(mt + 1) * P, half * HALF:(half + 1) * HALF], in_=results[half, mt][:])
+
+        load_scales(1, 0)
+        load_g(1, 0)
+        load_u(0)
+        load_g(1, 1)
+        load_u(1)
+        load_g(1, 2)
+        load_scales(1, 1)
+        load_g(1, 3)
+        store(0, 0)
+        load_g(1, 4)
+        load_u(2)
+        load_g(1, 5)
+        load_u(3)
+        load_g(1, 6)
+        load_g(1, 7)
+        for mt in range(1, MT):
+            store(0, mt)
+
+        for mt, nt in banks:
+            accs[mt, nt] = psum.tile([P, NT], F32, name="acc%d_%d" % (mt, nt))
+        for g in range(TOGETHER):
+            for mt, nt in banks:
+                multiply(accs[mt, nt], 1, g, mt, nt)
+        for mt, nt in banks:
+            for g in range(TOGETHER, H):
+                multiply(accs[mt, nt], 1, g, mt, nt)
+            dst = results[1, mt][:, nt * NT:(nt + 1) * NT]
+            nc.vector.scalar_tensor_tensor(
+                out=dst, in0=accs[mt, nt][:], scalar=cr[:, mt:mt + 1], in1=dst, op0=MULT, op1=ADD
+            )
+            if mt == MT - 1:
+                nc.sync.dma_start(out=out[mt * P:(mt + 1) * P, HALF + nt * NT:HALF + (nt + 1) * NT], in_=dst)
+            elif nt == 1:
+                store(1, mt)

@@ -22,7 +22,7 @@ MT = M // P
 NT = 512
 HALF = N // 2
 MH = M // 2
-SCALE_RUNS = (((0, 3), (3, 8)), ((0, 4), (4, 8)))
+SCALE_RUNS = (((0, 4), (4, 8)), ((0, 4), (4, 8)))
 TOGETHER = 6
 
 
@@ -40,26 +40,33 @@ def tile_held_control_gradient_e2_kernel(tc, g_words, g_scales, jac, c, r, u, ou
         for half in range(2):
             for g0, g1 in SCALE_RUNS[half]:
                 plane = keep.tile([P, g1 - g0, HALF], U8, name="plane%d_%d" % (half, g0), align_bytes=64)
-                nc.vector.memset(plane[:].bitcast(I32), 0)
+                if half == 0:
+                    nc.vector.memset(plane[:].bitcast(I32), 0)
                 for g in range(g0, g1):
                     planes[half, g] = (plane, g - g0)
-        cr_rows = keep.tile([P, 32], BF16, name="cr_rows", align_bytes=64)
+        cr_rows = keep.tile([P, P], BF16, name="cr_rows", align_bytes=64)
         nc.vector.memset(cr_rows[:], 0.0)
 
-        def load_scales(half, run):
+        def load_scales(half, run, rows=range(4)):
             g0, g1 = SCALE_RUNS[half][run]
             plane = planes[half, g0][0]
             words = slice(half * HALF // 4, (half + 1) * HALF // 4)
-            for s in range(4):
+            for s in rows:
                 nc.sync.dma_start(out=plane[s:P:32, :, :].bitcast(I32), in_=scale_rows[s, :, g0:g1, words])
 
         g_codes = {}
 
-        def load_g(half, g):
-            codes = keep.tile([P, HALF], U32, name="g%d_%d" % (half, g), align_bytes=64)
-            src = g_words[g].rearrange("p n t -> p (n t)")[:, half * HALF * PACK:(half + 1) * HALF * PACK]
-            nc.sync.dma_start(out=codes[:].bitcast(I32), in_=src.bitcast(I32))
-            g_codes[half, g] = codes
+        g_rows = g_words.rearrange("g p n t -> p g (n t)").bitcast(I32)
+
+        def load_g(half, g0, g1, width=HALF):
+            codes = keep.tile([P, g1 - g0, HALF], U32, name="g%d_%d" % (half, g0), align_bytes=64)
+            for n0 in range(0, HALF, width):
+                nc.sync.dma_start(
+                    out=codes[:, :, n0:n0 + width].bitcast(I32),
+                    in_=g_rows[:, g0:g1, half * HALF + n0:half * HALF + n0 + width],
+                )
+            for g in range(g0, g1):
+                g_codes[half, g] = codes[:, g - g0, :]
 
         raws = {}
 
@@ -68,9 +75,12 @@ def tile_held_control_gradient_e2_kernel(tc, g_words, g_scales, jac, c, r, u, ou
             nc.sync.dma_start(out=raw[:], in_=jac[g].rearrange("(p j) m -> p j m", j=PACK))
             raws[g] = raw
 
-        def load_cr(t):
-            nc.sync.dma_start(out=cr_rows[t:P:32, :], in_=c.rearrange("(t q j) -> t q j", t=MT, q=4)[t])
-            nc.sync.dma_start(out=cr_rows[MT + t:P:32, :], in_=r.rearrange("(t q j) -> t q j", t=MT, q=4)[t])
+        def load_cr():
+            for row, vec in enumerate((c, r)):
+                nc.sync.dma_start(
+                    out=cr_rows[row:P:32, :].rearrange("q (t j) -> q t j", t=MT),
+                    in_=vec.rearrange("(t q j) -> q t j", t=MT, q=4),
+                )
 
         b_codes = {}
 
@@ -78,12 +88,12 @@ def tile_held_control_gradient_e2_kernel(tc, g_words, g_scales, jac, c, r, u, ou
             grouped = []
             for mh in range(2):
                 tile = stage.tile([P, MH, PACK], BF16, name="grouped%d" % mh, align_bytes=64)
-                dst = tile[:].rearrange("p (a i) j -> p a j i", i=4)
-                src = raws[g][:, :, mh * MH:(mh + 1) * MH].rearrange("p j (a i) -> p a j i", i=4)
+                dst = tile[:]
+                src = raws[g][:, :, mh * MH:(mh + 1) * MH].rearrange("p j m -> p m j")
                 if mh == 0:
                     nc.vector.tensor_copy(out=dst, in_=src)
                 else:
-                    nc.scalar.activation(out=dst, in_=src, func=COPY)
+                    nc.scalar.copy(out=dst, in_=src)
                 grouped.append(tile)
             for mh in range(2):
                 codes = keep.tile([P, MH], U32, name="bc%d_%d" % (g, mh), align_bytes=64)
@@ -115,64 +125,69 @@ def tile_held_control_gradient_e2_kernel(tc, g_words, g_scales, jac, c, r, u, ou
         accs = {}
         for mt, nt in banks:
             accs[mt, nt] = psum.tile([P, NT], F32, name="acc%d_%d" % (mt, nt))
-        cr_cols = keep.tile([P, 32], BF16, name="cr_cols", align_bytes=64)
-        cr = keep.tile([P, 2 * MT], F32, name="cr")
+        cr_cols = keep.tile([P, P], BF16, name="cr_cols", align_bytes=64)
+        cr = keep.tile([P, 2, MT], F32, name="cr")
         for g in range(H):
             load_jac(g)
+            load_g(0, g, g + 1)
             if g == 0:
                 load_scales(0, 0)
-            load_g(0, g)
-            if g == 1:
                 load_scales(0, 1)
-            if 2 <= g < 2 + MT:
-                load_cr(g - 2)
+            if g == 3:
+                load_cr()
             quantize_jac(g)
-            if g == H - 1:
+            if g in (2, 4):
+                nc.vector.memset(planes[1, SCALE_RUNS[1][g // 2 - 1][0]][0][:].bitcast(I32), 0)
+            if g == H - 2:
                 nc.vector.transpose(out=cr_cols[:], in_=cr_rows[:])
-                nc.vector.tensor_copy(out=cr[:], in_=cr_cols[:, 0:2 * MT])
+                nc.vector.tensor_copy(out=cr[:], in_=cr_cols[:].rearrange("p (t i) -> p i t", t=MT)[:, 0:2, :])
             for mt, nt in banks:
                 multiply(accs[mt, nt], 0, g, mt, nt)
 
         results = {}
+        pairs = {}
         for half in range(2):
-            for mt in range(MT):
-                results[half, mt] = keep.tile([P, HALF], F32, name="res%d_%d" % (half, mt))
+            for mh in range(2):
+                pairs[half, mh] = keep.tile([P, 2, HALF], F32, name="res%d_%d" % (half, mh))
+                for i in range(2):
+                    results[half, 2 * mh + i] = pairs[half, mh][:, i, :]
         for mt, nt in banks:
             dst = results[0, mt][:, nt * NT:(nt + 1) * NT]
-            if nt == 0:
-                nc.scalar.activation(out=dst, in_=accs[mt, nt][:], func=COPY, scale=cr[:, mt:mt + 1])
+            if mt >= MT // 2:
+                nc.scalar.activation(out=dst, in_=accs[mt, nt][:], func=COPY, scale=cr[:, 0, mt:mt + 1])
             else:
-                nc.vector.tensor_scalar(out=dst, in0=accs[mt, nt][:], scalar1=cr[:, mt:mt + 1], scalar2=None, op0=MULT)
+                nc.vector.tensor_scalar(out=dst, in0=accs[mt, nt][:], scalar1=cr[:, 0, mt:mt + 1], scalar2=None, op0=MULT)
 
-        def load_u(mt):
-            u_rows = keep.tile([P, N], BF16, name="u%d" % mt)
-            nc.sync.dma_start(out=u_rows[:], in_=u[mt * P:(mt + 1) * P, :])
-            r_col = cr[:, MT + mt:MT + mt + 1]
-            nc.vector.scalar_tensor_tensor(
-                out=results[0, mt][:], in0=u_rows[:, 0:HALF], scalar=r_col, in1=results[0, mt][:], op0=MULT, op1=ADD
-            )
-            nc.scalar.activation(out=results[1, mt][:], in_=u_rows[:, HALF:N], func=COPY, scale=r_col)
+        def load_u(half, mt0, mt1):
+            rows = keep.tile([P, mt1 - mt0, HALF], BF16, name="u%d_%d" % (half, mt0))
+            src = u[mt0 * P:mt1 * P, half * HALF:(half + 1) * HALF].rearrange("(i p) n -> p i n", p=P)
+            nc.sync.dma_start(out=rows[:], in_=src)
+            for mt in range(mt0, mt1):
+                r_col = cr[:, 1, mt:mt + 1]
+                if half == 0:
+                    nc.vector.scalar_tensor_tensor(
+                        out=results[0, mt], in0=rows[:, mt - mt0, :], scalar=r_col, in1=results[0, mt], op0=MULT, op1=ADD
+                    )
+                else:
+                    nc.scalar.activation(out=results[1, mt], in_=rows[:, mt - mt0, :], func=COPY, scale=r_col)
 
-        def store(half, mt):
-            nc.sync.dma_start(out=out[mt * P:(mt + 1) * P, half * HALF:(half + 1) * HALF], in_=results[half, mt][:])
+        def store(half, mt, n0, n1):
+            nc.sync.dma_start(out=out[mt * P:(mt + 1) * P, half * HALF + n0:half * HALF + n1], in_=results[half, mt][:, n0:n1])
 
         load_scales(1, 0)
-        load_g(1, 0)
-        load_u(0)
-        load_g(1, 1)
-        load_u(1)
-        load_g(1, 2)
-        load_scales(1, 1)
-        load_g(1, 3)
-        store(0, 0)
-        load_g(1, 4)
-        load_u(2)
-        load_g(1, 5)
-        load_u(3)
-        load_g(1, 6)
-        load_g(1, 7)
-        for mt in range(1, MT):
-            store(0, mt)
+        for g in range(4):
+            load_g(1, g, g + 1)
+            load_scales(1, 1, [g])
+        load_g(1, 4, 5)
+        load_u(0, 0, MT)
+        load_g(1, 5, 6)
+        load_u(1, 0, 2)
+        load_g(1, 6, 8)
+        load_u(1, 2, MT)
+        for mh in range(2):
+            nc.sync.dma_start(
+                out=out[mh * MH:(mh + 1) * MH, 0:HALF].rearrange("(i p) n -> p i n", p=P), in_=pairs[0, mh][:]
+            )
 
         for mt, nt in banks:
             accs[mt, nt] = psum.tile([P, NT], F32, name="acc%d_%d" % (mt, nt))
@@ -184,9 +199,9 @@ def tile_held_control_gradient_e2_kernel(tc, g_words, g_scales, jac, c, r, u, ou
                 multiply(accs[mt, nt], 1, g, mt, nt)
             dst = results[1, mt][:, nt * NT:(nt + 1) * NT]
             nc.vector.scalar_tensor_tensor(
-                out=dst, in0=accs[mt, nt][:], scalar=cr[:, mt:mt + 1], in1=dst, op0=MULT, op1=ADD
+                out=dst, in0=accs[mt, nt][:], scalar=cr[:, 0, mt:mt + 1], in1=dst, op0=MULT, op1=ADD
             )
             if mt == MT - 1:
-                nc.sync.dma_start(out=out[mt * P:(mt + 1) * P, HALF + nt * NT:HALF + (nt + 1) * NT], in_=dst)
+                store(1, mt, nt * NT, (nt + 1) * NT)
             elif nt == 1:
-                store(1, mt)
+                store(1, mt, 0, HALF)

from contextlib import ExitStack

import concourse.mybir as mybir

H, D, M, N = 8, 512, 512, 2048
FLOPS = 2 * H * D * M * N

F32 = mybir.dt.float32
BF16 = mybir.dt.bfloat16
I32 = mybir.dt.int32
U32 = mybir.dt.uint32
U8 = mybir.dt.uint8
E4M3 = mybir.dt.float8_e4m3fn_x4
E5M2 = mybir.dt.float8_e5m2_x4
COPY = mybir.ActivationFunctionType.Copy
MULT = mybir.AluOpType.mult
ADD = mybir.AluOpType.add

P = 128
PACK = 4
MT = M // P
NT = 512
HALF = N // 2
MH = M // 2
SCALE_RUNS = (((0, 4), (4, 8)), ((0, 4), (4, 8)))
TOGETHER = 6


def tile_held_control_gradient_e2_kernel(tc, g_words, g_scales, jac, c, r, u, out):
    nc = tc.nc
    with ExitStack() as ctx:
        keep = ctx.enter_context(tc.tile_pool(name="keep", bufs=1))
        stage = ctx.enter_context(tc.tile_pool(name="stage", bufs=3))
        psum = ctx.enter_context(tc.psum_pool(name="psum", bufs=1))
        ctx.enter_context(tc.manual_schedule())

        scale_rows = g_scales.bitcast(I32).rearrange("g (q s) n -> s q g n", s=4)

        planes = {}
        for half in range(2):
            for g0, g1 in SCALE_RUNS[half]:
                plane = keep.tile([P, g1 - g0, HALF], U8, name="plane%d_%d" % (half, g0), align_bytes=64)
                if half == 0:
                    nc.vector.memset(plane[:].bitcast(I32), 0)
                for g in range(g0, g1):
                    planes[half, g] = (plane, g - g0)
        cr_rows = keep.tile([P, P], BF16, name="cr_rows", align_bytes=64)
        nc.vector.memset(cr_rows[:], 0.0)

        def load_scales(half, run, rows=range(4)):
            g0, g1 = SCALE_RUNS[half][run]
            plane = planes[half, g0][0]
            words = slice(half * HALF // 4, (half + 1) * HALF // 4)
            for s in rows:
                nc.sync.dma_start(out=plane[s:P:32, :, :].bitcast(I32), in_=scale_rows[s, :, g0:g1, words])

        g_codes = {}

        g_rows = g_words.rearrange("g p n t -> p g (n t)").bitcast(I32)

        def load_g(half, g0, g1, width=HALF):
            codes = keep.tile([P, g1 - g0, HALF], U32, name="g%d_%d" % (half, g0), align_bytes=64)
            for n0 in range(0, HALF, width):
                nc.sync.dma_start(
                    out=codes[:, :, n0:n0 + width].bitcast(I32),
                    in_=g_rows[:, g0:g1, half * HALF + n0:half * HALF + n0 + width],
                )
            for g in range(g0, g1):
                g_codes[half, g] = codes[:, g - g0, :]

        raws = {}

        def load_jac(g):
            raw = keep.tile([P, PACK, M], BF16, name="raw%d" % g)
            nc.sync.dma_start(out=raw[:], in_=jac[g].rearrange("(p j) m -> p j m", j=PACK))
            raws[g] = raw

        def load_cr():
            for row, vec in enumerate((c, r)):
                nc.sync.dma_start(
                    out=cr_rows[row:P:32, :].rearrange("q (t j) -> q t j", t=MT),
                    in_=vec.rearrange("(t q j) -> q t j", t=MT, q=4),
                )

        b_codes = {}

        def quantize_jac(g):
            grouped = []
            for mh in range(2):
                tile = stage.tile([P, MH, PACK], BF16, name="grouped%d" % mh, align_bytes=64)
                dst = tile[:]
                src = raws[g][:, :, mh * MH:(mh + 1) * MH].rearrange("p j m -> p m j")
                if mh == 0:
                    nc.vector.tensor_copy(out=dst, in_=src)
                else:
                    nc.scalar.copy(out=dst, in_=src)
                grouped.append(tile)
            for mh in range(2):
                codes = keep.tile([P, MH], U32, name="bc%d_%d" % (g, mh), align_bytes=64)
                scales = keep.tile([P, MH], U8, name="bs%d_%d" % (g, mh), align_bytes=64)
                nc.vector.quantize_mx(
                    out=codes[:].bitcast(E4M3),
                    scales=scales[:],
                    in_=grouped[mh][:].rearrange("p m j -> p (m j)"),
                )
                b_codes[g, mh] = (codes, scales)

        def multiply(acc, half, g, mt, nt):
            codes, scales = b_codes[g, mt // 2]
            m_cols = slice((mt % 2) * P, (mt % 2 + 1) * P)
            n_cols = slice(nt * NT, (nt + 1) * NT)
            plane, slot = planes[half, g]
            nc.tensor.matmul_mx(
                out=acc[:],
                lhsT=codes[:, m_cols].bitcast(E4M3),
                lhsT_scale=scales[:, m_cols],
                rhs=g_codes[half, g][:, n_cols].bitcast(E5M2),
                rhs_scale=plane[:, slot, n_cols],
                start=(g == 0),
                stop=(g == H - 1),
            )

        banks = [(mt, nt) for mt in range(MT) for nt in range(2)]

        accs = {}
        for mt, nt in banks:
            accs[mt, nt] = psum.tile([P, NT], F32, name="acc%d_%d" % (mt, nt))
        cr_cols = keep.tile([P, P], BF16, name="cr_cols", align_bytes=64)
        cr = keep.tile([P, 2, MT], F32, name="cr")
        for g in range(H):
            load_jac(g)
            load_g(0, g, g + 1)
            if g == 0:
                load_scales(0, 0)
                load_scales(0, 1)
            if g == 3:
                load_cr()
            quantize_jac(g)
            if g in (2, 4):
                nc.vector.memset(planes[1, SCALE_RUNS[1][g // 2 - 1][0]][0][:].bitcast(I32), 0)
            if g == H - 2:
                nc.vector.transpose(out=cr_cols[:], in_=cr_rows[:])
                nc.vector.tensor_copy(out=cr[:], in_=cr_cols[:].rearrange("p (t i) -> p i t", t=MT)[:, 0:2, :])
            for mt, nt in banks:
                multiply(accs[mt, nt], 0, g, mt, nt)

        results = {}
        pairs = {}
        for half in range(2):
            for mh in range(2):
                pairs[half, mh] = keep.tile([P, 2, HALF], F32, name="res%d_%d" % (half, mh))
                for i in range(2):
                    results[half, 2 * mh + i] = pairs[half, mh][:, i, :]
        for mt, nt in banks:
            dst = results[0, mt][:, nt * NT:(nt + 1) * NT]
            if mt >= MT // 2:
                nc.scalar.activation(out=dst, in_=accs[mt, nt][:], func=COPY, scale=cr[:, 0, mt:mt + 1])
            else:
                nc.vector.tensor_scalar(out=dst, in0=accs[mt, nt][:], scalar1=cr[:, 0, mt:mt + 1], scalar2=None, op0=MULT)

        def load_u(half, mt0, mt1):
            rows = keep.tile([P, mt1 - mt0, HALF], BF16, name="u%d_%d" % (half, mt0))
            src = u[mt0 * P:mt1 * P, half * HALF:(half + 1) * HALF].rearrange("(i p) n -> p i n", p=P)
            nc.sync.dma_start(out=rows[:], in_=src)
            for mt in range(mt0, mt1):
                r_col = cr[:, 1, mt:mt + 1]
                if half == 0:
                    nc.vector.scalar_tensor_tensor(
                        out=results[0, mt], in0=rows[:, mt - mt0, :], scalar=r_col, in1=results[0, mt], op0=MULT, op1=ADD
                    )
                else:
                    nc.scalar.activation(out=results[1, mt], in_=rows[:, mt - mt0, :], func=COPY, scale=r_col)

        def store(half, mt, n0, n1):
            nc.sync.dma_start(out=out[mt * P:(mt + 1) * P, half * HALF + n0:half * HALF + n1], in_=results[half, mt][:, n0:n1])

        load_scales(1, 0)
        for g in range(4):
            load_g(1, g, g + 1)
            load_scales(1, 1, [g])
        load_g(1, 4, 5)
        load_u(0, 0, MT)
        load_g(1, 5, 6)
        load_u(1, 0, 2)
        load_g(1, 6, 8)
        load_u(1, 2, MT)
        for mh in range(2):
            nc.sync.dma_start(
                out=out[mh * MH:(mh + 1) * MH, 0:HALF].rearrange("(i p) n -> p i n", p=P), in_=pairs[0, mh][:]
            )

        for mt, nt in banks:
            accs[mt, nt] = psum.tile([P, NT], F32, name="acc%d_%d" % (mt, nt))
        for g in range(TOGETHER):
            for mt, nt in banks:
                multiply(accs[mt, nt], 1, g, mt, nt)
        for mt, nt in banks:
            for g in range(TOGETHER, H):
                multiply(accs[mt, nt], 1, g, mt, nt)
            dst = results[1, mt][:, nt * NT:(nt + 1) * NT]
            nc.vector.scalar_tensor_tensor(
                out=dst, in0=accs[mt, nt][:], scalar=cr[:, 0, mt:mt + 1], in1=dst, op0=MULT, op1=ADD
            )
            if mt == MT - 1:
                store(1, mt, nt * NT, (nt + 1) * NT)
            elif nt == 1:
                store(1, mt, 0, HALF)
